import numpy as np
import ml_dtypes


def mxq(x, axis, fmt="e4m3"):
    dtype, down = {"e4m3": (ml_dtypes.float8_e4m3fn, 7), "e5m2": (ml_dtypes.float8_e5m2, 14)}[fmt]
    v = np.moveaxis(np.asarray(x, np.float32).astype(ml_dtypes.bfloat16).astype(np.float64), axis, -1)
    blocks = v.reshape(v.shape[:-1] + (-1, 32))
    amax = np.abs(blocks).max(-1, keepdims=True)
    byte = np.maximum(np.where(amax > 0, np.frexp(amax)[1] - 1 + 127, 0) - down, 1)
    scale = np.exp2(byte - 127.0)
    codes = (blocks / scale).astype(np.float32).astype(dtype).astype(np.float64)
    return np.moveaxis((codes * scale).reshape(v.shape), -1, axis)


WIDE = False


def mx_kscale(k):
    if not WIDE:
        return np.ones(k)
    levels = np.array([30, -30])
    if k % 512:
        return np.exp2(np.random.permutation(np.resize(levels, k // 32))).repeat(32)
    a = np.empty((k // 512, 16))
    for p in range(k // 512):
        a[p, :8] = np.random.permutation(np.resize(levels, 8))
        for g in range(8):
            far = levels[np.abs(levels - a[p, g]) >= 10]
            a[p, g + 8] = far[np.random.randint(len(far))]
    return np.exp2(a.ravel()).repeat(32)


def f64(x):
    return np.asarray(x).astype(np.float64)


def striped(idx):
    return np.tile(np.asarray(idx).reshape(-1, 16).T, (8, 1)).astype(np.uint16)


def unstriped(offs):
    return offs[:16].T.reshape(-1).astype(np.int64)


E2M1 = np.array([0.0, 0.5, 1.0, 1.5, 2.0, 3.0, 4.0, 6.0, -0.0, -0.5, -1.0, -1.5, -2.0, -3.0, -4.0, -6.0])


def pack_weight(w, fmt):
    k, n = w.shape
    w = f64(np.asarray(w, np.float32).astype(ml_dtypes.bfloat16)).reshape(k // 32, 32, n)
    amax = np.abs(w).max(1)
    if fmt in ("e4m3", "e5m2"):
        byte = np.frexp(amax)[1] - 1 + 127 - (7 if fmt == "e4m3" else 14)
    else:
        mant, ex = np.frexp(amax / 6.0)
        byte = np.where(mant > 0.5, ex, ex - 1) + 127
    byte = np.clip(np.where(amax > 0, byte, 1), 1, 254)
    scaled = (w * np.exp2(127.0 - byte)[:, None, :]).reshape(k, n).astype(np.float32)
    by_word = np.ascontiguousarray(scaled.reshape(k // 512, 128, 4, n).transpose(0, 1, 3, 2))
    if fmt in ("e4m3", "e5m2"):
        words = by_word.astype(ml_dtypes.float8_e4m3fn if fmt == "e4m3" else ml_dtypes.float8_e5m2).view(np.uint8)
    else:
        c = by_word.astype(ml_dtypes.float4_e2m1fn).view(np.uint8) & 0xF
        words = (c[..., 0::2] | (c[..., 1::2] << 4)).reshape(k // 512, 128, 2 * n)
    return np.ascontiguousarray(words), np.ascontiguousarray(byte.astype(np.uint8).reshape(k // 512, 16, n))


def unpack_weight(words, scales, fmt):
    g, _, n = scales.shape
    words = np.ascontiguousarray(words).reshape(g, 128, n, -1)
    if fmt in ("e4m3", "e5m2"):
        vals = words.view(ml_dtypes.float8_e4m3fn if fmt == "e4m3" else ml_dtypes.float8_e5m2).astype(np.float64)
    else:
        nib = np.empty((g, 128, n, 4), np.uint8)
        nib[..., 0::2] = words & 0xF
        nib[..., 1::2] = words >> 4
        vals = E2M1[nib]
    vals = vals * np.repeat(np.exp2(scales.astype(np.float64) - 127.0), 8, axis=1)[..., None]
    return vals.transpose(0, 1, 3, 2).reshape(g * 512, n)


def bf(x):
    return np.asarray(x, np.float32).astype(ml_dtypes.bfloat16)


def planes(Y):
    r, m = Y.shape
    b = f64(bf(Y)).reshape(r // 32, 32, m)
    amax = np.abs(b).max(1)
    byte = np.clip(np.where(amax > 0, np.frexp(amax)[1] - 1 + 127 - 7, 1), 1, 254)
    codes = (b * np.exp2(127.0 - byte)[:, None, :]).reshape(r, m).astype(np.float32).astype(ml_dtypes.float8_e4m3fn).view(np.uint8)
    words = codes.reshape(r // 512, 128, 4, m).transpose(0, 1, 3, 2)
    return np.ascontiguousarray(words), np.ascontiguousarray(byte.astype(np.uint8).reshape(r // 512, 16, m))


K, T, J, S, R, F, V, N, C = 512, 512, 256, 512, 512, 512, 512, 512, 512


def setup_inputs():
    n = np.random.standard_normal
    idx = np.random.permutation(T)[:J]
    idx2 = np.random.permutation(S)[:J]
    idx3 = np.random.permutation(V)[:J]
    idx4 = np.random.permutation(C)[:J]
    fk = mx_kscale(K)
    fr = mx_kscale(R)
    ff = mx_kscale(F)
    wp = pack_weight(n((K, R)) * 1 / np.sqrt(K) * fk[:, None] * fr, "e4m3")
    sxp = pack_weight(n((F, J)) / ff[:, None], "e2m1")
    w2p = pack_weight(n((F, R)) * 1 / np.sqrt(F) * ff[:, None] * fr, "e5m2")
    wbp = pack_weight(n((R, N)) * 1 / np.sqrt(R) / fr[:, None], "e2m1")
    return {
        "xa": (n((K, T))).astype(np.float32),
        "xb": (n((K, S))).astype(np.float32),
        "hb": (np.random.uniform(0.2, 0.9, (K, 1))).astype(np.float32),
        "fk": (np.random.uniform(0.5, 2.0, (K, 1)) / fk[:, None]).astype(np.float32),
        "w_words": wp[0],
        "w_scales": wp[1],
        "sx_words": sxp[0],
        "sx_scales": sxp[1],
        "w2_words": w2p[0],
        "w2_scales": w2p[1],
        "tb": (n((R, V)) * 0.7).astype(np.float32),
        "wb_words": wbp[0],
        "wb_scales": wbp[1],
        "tz": (n((N, C)) * 0.6).astype(np.float32),
        "rw": (np.random.uniform(0.5, 2.0, (1, J))).astype(np.float32),
        "offs": striped(idx),
        "offs2": striped(idx2),
        "offs3": striped(idx3),
        "offs4": striped(idx4),
    }


def reference(xa, xb, hb, fk, w_words, w_scales, sx_words, sx_scales, w2_words, w2_scales, tb, wb_words, wb_scales, tz, rw, offs, offs2, offs3, offs4):
    idx = unstriped(offs)
    idx2 = unstriped(offs2)
    idx3 = unstriped(offs3)
    idx4 = unstriped(offs4)
    wu = unpack_weight(w_words, w_scales, "e4m3")
    sxu = unpack_weight(sx_words, sx_scales, "e2m1")
    w2u = unpack_weight(w2_words, w2_scales, "e5m2")
    wbu = unpack_weight(wb_words, wb_scales, "e2m1")
    u = (f64(xa)[:, idx] - np.minimum(f64(xb)[:, idx2], f64(hb))) * f64(fk)
    uq = mxq(u, 0, "e4m3")
    a = wu.T @ uq + w2u.T @ sxu
    hid = np.maximum(a, 0.0) * f64(tb)[:, idx3]
    hidq = mxq(hid, 0, "e5m2")
    p = wbu.T @ hidq
    y = np.maximum(p, f64(tz)[:, idx4]) * f64(rw)
    words, scales = planes(y)
    return y, words, scales

from contextlib import ExitStack

import concourse.mybir as mybir
from concourse.masks import make_identity

F32 = mybir.dt.float32
BF16 = mybir.dt.bfloat16
I32 = mybir.dt.int32
U32 = mybir.dt.uint32
U16 = mybir.dt.uint16
U8 = mybir.dt.uint8
E4M3 = mybir.dt.float8_e4m3fn_x4
E5M2 = mybir.dt.float8_e5m2_x4
E2M1 = mybir.dt.float4_e2m1fn_x4
ALU = mybir.AluOpType
COPY = mybir.ActivationFunctionType.Copy

P = 128
PACK = 4
ROWS = 512
COLS = 512
J = 256
HALF = 128
HALVES = J // HALF
FLOPS = 3 * 2 * ROWS * ROWS * J


def tile_list_sum_boundedgaps_own_timestable_floored_pl_kernel(
    tc, xa, xb, hb, fk, w_words, w_scales, sx_words, sx_scales, w2_words, w2_scales, tb,
    wb_words, wb_scales, tz, rw, offs, offs2, offs3, offs4, out_0, out_1, out_2,
):
    nc = tc.nc
    with ExitStack() as ctx:
        lists = ctx.enter_context(tc.tile_pool(name="lists", bufs=1))
        sb = ctx.enter_context(tc.tile_pool(name="sb", bufs=1))
        ps = ctx.enter_context(tc.psum_pool(name="ps", bufs=1))

        def load_list(name, src):
            tile = lists.tile([P, J // 16], U16, name=name)
            nc.sync.dma_start(tile[:], src)
            return tile

        def load_planes(name, src, first, count):
            tile = sb.tile([P, count, COLS], F32, name=name)
            nc.sync.dma_start(tile[:], src.rearrange("(p t) c -> p t c", t=PACK)[:, first : first + count, :])
            return [tile[:, i, :] for i in range(count)]

        def load_scale_rows(eng, tile, row, src):
            for q in range(4):
                eng.dma_start(tile[32 * q + row : 32 * q + row + 4, :].bitcast(I32), src[0, 4 * q : 4 * q + 4, :].bitcast(I32))

        def load_bytes(name, src, width):
            tile = sb.tile([P, width], U8, name=name, align_bytes=64)
            nc.sync.dma_start(tile[:].bitcast(I32), src.bitcast(I32))
            return tile

        def gather_s(out, window, offsets):
            nc.scalar.activation(out, window.indirect(offsets), COPY)

        def gather_v(out, window, offsets):
            nc.vector.tensor_copy(out, window.indirect(offsets))

        def deal(copy, out, src):
            copy(out.rearrange("p (t m) -> p t m", t=PACK), src.rearrange("p (m t) -> p t m", t=PACK))


        scale_raw = sb.tile([P, 2 * ROWS + J], U8, name="scale_raw", align_bytes=64)
        nc.vector.memset(scale_raw[:].bitcast(I32), 0)
        s1_raw = scale_raw[:, 0:ROWS]
        sb_raw = scale_raw[:, ROWS : 2 * ROWS]
        sx_s = scale_raw[:, 2 * ROWS : 2 * ROWS + J]
        ident = sb.tile([P, P], F32, name="ident")
        make_identity(nc, ident[:])

        l2 = load_list("l2", offs2)
        xb_p = load_planes("xb01", xb, 0, 2)
        hb_t = sb.tile([P, PACK], F32, name="hb_t")
        nc.sync.dma_start(hb_t[:], hb.rearrange("(p t) o -> p (t o)", t=PACK))
        l1 = load_list("l1", offs)
        xa_p = load_planes("xa01", xa, 0, 2)
        fk_t = sb.tile([P, PACK], F32, name="fk_t")
        nc.sync.dma_start(fk_t[:], fk.rearrange("(p t) o -> p (t o)", t=PACK))
        xb_p = xb_p + load_planes("xb23", xb, 2, 2)
        load_scale_rows(nc.sync, s1_raw, 0, w2_scales)
        xa_p = xa_p + load_planes("xa23", xa, 2, 2)
        load_scale_rows(nc.sync, s1_raw, 4, w_scales)
        w2_raw = load_bytes("w2_raw", w2_words[0].rearrange("p c t -> p (c t)"), 4 * ROWS)
        w_raw = load_bytes("w_raw", w_words[0].rearrange("p c t -> p (c t)"), 4 * ROWS)
        sx_w = load_bytes("sx_w", sx_words[0], 2 * J)
        l3 = load_list("l3", offs3)
        tb_p = load_planes("tb01", tb, 0, 2)
        load_scale_rows(nc.sync, sx_s, 0, sx_scales)
        tb_p = tb_p + load_planes("tb23", tb, 2, 2)
        wb_raw = load_bytes("wb_raw", wb_words[0], 2 * ROWS)
        load_scale_rows(nc.sync, sb_raw, 0, wb_scales)
        l4 = load_list("l4", offs4)
        tz_p = load_planes("tz01", tz, 0, 2)
        rw_col = sb.tile([P, HALVES], F32, name="rw_col")
        with nc.allow_non_contiguous_dma(reason="one weight a partition and half"):
            nc.sync.dma_start(rw_col[:], rw.rearrange("o (h p) -> p (o h)", p=P))
        tz_p = tz_p + load_planes("tz2", tz, 2, 1)
        tz_p = tz_p + load_planes("tz3", tz, 3, 1)

        neg_fk = sb.tile([P, PACK], F32, name="neg_fk")
        xa_g = sb.tile([P, PACK, J], F32, name="xa_g")
        xb_g = sb.tile([P, PACK, J], F32, name="xb_g")
        gap = sb.tile([P, PACK, J], F32, name="gap")
        for t in range(PACK):
            gather_s(xb_g[:, t, :], xb_p[t], l2[:])
            gather_v(xa_g[:, t, :], xa_p[t], l1[:])
            if t == 0:
                nc.vector.tensor_scalar(neg_fk[:], fk_t[:], -1.0, None, ALU.mult)
            nc.vector.scalar_tensor_tensor(gap[:, t, :], xb_g[:, t, :], hb_t[:, t : t + 1], xa_g[:, t, :], ALU.min, ALU.subtract)

        s1 = sb.tile([P, ROWS], U8, name="s1", align_bytes=64)
        deal(nc.vector.tensor_copy, s1[:], s1_raw)
        w2_d = sb.tile([P, ROWS], U32, name="w2_d", align_bytes=64)
        deal(nc.scalar.copy, w2_d[:], w2_raw[:].bitcast(U32))
        w_d = sb.tile([P, ROWS], U32, name="w_d", align_bytes=64)
        deal(nc.scalar.copy, w_d[:], w_raw[:].bitcast(U32))

        u_b, u_q, u_s = [], [], []
        for h in range(HALVES):
            u_b.append(sb.tile([P, HALF, PACK], BF16, name="u_b%d" % h, align_bytes=64))
            u_q.append(sb.tile([P, HALF], U32, name="u_q%d" % h, align_bytes=64))
            u_s.append(sb.tile([P, HALF], U8, name="u_s%d" % h, align_bytes=64))
        for h in range(HALVES):
            cols = slice(h * HALF, (h + 1) * HALF)
            nc.vector.tensor_tensor(
                u_b[h][:].rearrange("p (c i) t -> p c t i", i=4),
                gap[:, :, cols].rearrange("p t (c i) -> p c t i", i=4),
                neg_fk[:].unsqueeze(1).unsqueeze(3).to_broadcast([P, HALF // 4, PACK, 4]),
                ALU.mult,
            )
        for h in range(HALVES):
            nc.vector.quantize_mx(u_q[h][:].bitcast(E4M3), u_s[h][:], u_b[h][:].rearrange("p j t -> p (j t)"))

        acc = [ps.tile([P, PACK, HALF], F32, name="acc%d" % h) for h in range(HALVES)]
        for h in range(HALVES):
            for t in range(PACK):
                m = slice(t * P, (t + 1) * P)
                nc.tensor.matmul_mx(
                    acc[h][:, t, :], lhsT=w2_d[:, m].bitcast(E5M2), lhsT_scale=s1[:, m],
                    rhs=sx_w[:, 2 * h * HALF : 2 * (h + 1) * HALF].bitcast(E2M1), rhs_scale=sx_s[:, h * HALF : (h + 1) * HALF],
                    start=(t == 0), stop=False,
                )
        for h in range(HALVES):
            for t in range(PACK):
                m = slice(t * P, (t + 1) * P)
                nc.tensor.matmul_mx(
                    acc[h][:, t, :], lhsT=w_d[:, m].bitcast(E4M3), lhsT_scale=s1[4:P, m],
                    rhs=u_q[h][:].bitcast(E4M3), rhs_scale=u_s[h][:],
                    start=False, stop=(t == PACK - 1),
                )

        tb_g = sb.tile([P, PACK, J], F32, name="tb_g")
        for t in range(PACK):
            gather_s(tb_g[:, t, :], tb_p[t], l3[:])
        wb_d = sb.tile([P, ROWS], U16, name="wb_d", align_bytes=64)
        deal(nc.scalar.copy, wb_d[:], wb_raw[:].bitcast(U16))
        sbd = sb.tile([P, ROWS], U8, name="sbd", align_bytes=64)
        deal(nc.vector.tensor_copy, sbd[:], sb_raw)

        rw_ps = ps.tile([P, J], F32, name="rw_ps")
        for h in range(HALVES):
            nc.tensor.transpose(rw_ps[:, h * HALF : (h + 1) * HALF], rw_col[:, h : h + 1].to_broadcast([P, P]), ident[:])

        h_b, h_q, h_s = [], [], []
        for h in range(HALVES):
            h_b.append(sb.tile([P, HALF, PACK], BF16, name="h_b%d" % h, align_bytes=64))
            h_q.append(sb.tile([P, HALF], U32, name="h_q%d" % h, align_bytes=64))
            h_s.append(sb.tile([P, HALF], U8, name="h_s%d" % h, align_bytes=64))
        for h in range(HALVES):
            cols = slice(h * HALF, (h + 1) * HALF)
            nc.vector.scalar_tensor_tensor(
                h_b[h][:], acc[h][:].rearrange("p t j -> p j t"), 0.0,
                tb_g[:, :, cols].rearrange("p t j -> p j t"), ALU.max, ALU.mult,
            )
        for h in range(HALVES):
            nc.vector.quantize_mx(h_q[h][:].bitcast(E5M2), h_s[h][:], h_b[h][:].rearrange("p j t -> p (j t)"))

        prod = [ps.tile([P, PACK, HALF], F32, name="prod%d" % h) for h in range(HALVES)]
        wb_bytes = wb_d[:].bitcast(U8)
        for h in range(HALVES):
            for t in range(PACK):
                nc.tensor.matmul_mx(
                    prod[h][:, t, :], lhsT=wb_bytes[:, 2 * t * P : 2 * (t + 1) * P].bitcast(E2M1),
                    lhsT_scale=sbd[:, t * P : (t + 1) * P],
                    rhs=h_q[h][:].bitcast(E5M2), rhs_scale=h_s[h][:], start=True, stop=True,
                )

        tz_g = sb.tile([P, PACK, J], F32, name="tz_g")
        for t in range(PACK):
            gather_s(tz_g[:, t, :], tz_p[t], l4[:])

        y_q = sb.tile([P, J], U32, name="y_q", align_bytes=64)
        y_s = sb.tile([P, J], U8, name="y_s", align_bytes=64)
        out_rows = out_0.rearrange("(p t) j -> p t j", t=PACK)
        out_words = out_1[0].rearrange("p c t -> p (c t)").bitcast(I32)
        y_b = []
        for h in range(HALVES):
            cols = slice(h * HALF, (h + 1) * HALF)
            top = sb.tile([P, PACK, HALF], F32, name="top%d" % h)
            nc.vector.tensor_tensor(top[:], prod[h][:], tz_g[:, :, cols], ALU.max)
            y = sb.tile([P, PACK, HALF], F32, name="y%d" % h)
            nc.vector.tensor_tensor(y[:], top[:], rw_ps[:, cols].unsqueeze(1).to_broadcast([P, PACK, HALF]), ALU.mult)
            nc.sync.dma_start(out_rows[:, :, cols], y[:])
            y_b.append(sb.tile([P, HALF, PACK], BF16, name="y_b%d" % h, align_bytes=64))
            copy = nc.scalar.copy if h == 0 else nc.vector.tensor_copy
            copy(y_b[h][:].rearrange("p (c i) t -> p c t i", i=4), y[:].rearrange("p t (c i) -> p c t i", i=4))
        for h in range(HALVES):
            cols = slice(h * HALF, (h + 1) * HALF)
            nc.vector.quantize_mx(y_q[:, cols].bitcast(E4M3), y_s[:, cols], y_b[h][:].rearrange("p j t -> p (j t)"))
            nc.sync.dma_start(out_words[:, cols], y_q[:, cols].bitcast(I32))
        for q in range(4):
            eng = nc.sync if q % 2 == 0 else nc.scalar
            eng.dma_start(out_2[0, 4 * q : 4 * q + 4, :].bitcast(I32), y_s[32 * q : 32 * q + 4, :].bitcast(I32))
